import numpy as np
import ml_dtypes


def mxq(x, axis, fmt="e4m3"):
    dtype, down = {"e4m3": (ml_dtypes.float8_e4m3fn, 7), "e5m2": (ml_dtypes.float8_e5m2, 14)}[fmt]
    v = np.moveaxis(np.asarray(x, np.float32).astype(ml_dtypes.bfloat16).astype(np.float64), axis, -1)
    blocks = v.reshape(v.shape[:-1] + (-1, 32))
    amax = np.abs(blocks).max(-1, keepdims=True)
    byte = np.maximum(np.where(amax > 0, np.frexp(amax)[1] - 1 + 127, 0) - down, 1)
    scale = np.exp2(byte - 127.0)
    codes = (blocks / scale).astype(np.float32).astype(dtype).astype(np.float64)
    return np.moveaxis((codes * scale).reshape(v.shape), -1, axis)


WIDE = False


def mx_kscale(k):
    if not WIDE:
        return np.ones(k)
    levels = np.array([10, -10, 5, -5, 0])
    if k % 512:
        return np.exp2(np.random.permutation(np.resize(levels, k // 32))).repeat(32)
    a = np.empty((k // 512, 16))
    for p in range(k // 512):
        a[p, :8] = np.random.permutation(np.resize(levels, 8))
        for g in range(8):
            far = levels[np.abs(levels - a[p, g]) >= 10]
            a[p, g + 8] = far[np.random.randint(len(far))]
    return np.exp2(a.ravel()).repeat(32)


def f64(x):
    return np.asarray(x).astype(np.float64)


def striped(idx):
    return np.tile(idx.reshape(-1, 16).T, (8, 1)).astype(np.uint16)


def unstriped(offs):
    return offs[:16].T.reshape(-1).astype(np.int64)


E2M1 = np.array([0.0, 0.5, 1.0, 1.5, 2.0, 3.0, 4.0, 6.0, -0.0, -0.5, -1.0, -1.5, -2.0, -3.0, -4.0, -6.0])


def pack_weight(w, fmt):
    k, n = w.shape
    w = f64(np.asarray(w, np.float32).astype(ml_dtypes.bfloat16)).reshape(k // 32, 32, n)
    amax = np.abs(w).max(1)
    if fmt == "e4m3":
        byte = np.frexp(amax)[1] - 1 + 127 - 7
    else:
        mant, ex = np.frexp(amax / 6.0)
        byte = np.where(mant > 0.5, ex, ex - 1) + 127
    byte = np.clip(np.where(amax > 0, byte, 1), 1, 254)
    scaled = (w * np.exp2(127.0 - byte)[:, None, :]).reshape(k, n).astype(np.float32)
    by_word = np.ascontiguousarray(scaled.reshape(k // 512, 128, 4, n).transpose(0, 1, 3, 2))
    if fmt == "e4m3":
        words = by_word.astype(ml_dtypes.float8_e4m3fn).view(np.uint8)
    else:
        c = by_word.astype(ml_dtypes.float4_e2m1fn).view(np.uint8) & 0xF
        words = (c[..., 0::2] | (c[..., 1::2] << 4)).reshape(k // 512, 128, 2 * n)
    return np.ascontiguousarray(words), np.ascontiguousarray(byte.astype(np.uint8).reshape(k // 512, 16, n))


def unpack_weight(words, scales, fmt):
    g, _, n = scales.shape
    words = np.ascontiguousarray(words).reshape(g, 128, n, -1)
    if fmt == "e4m3":
        vals = words.view(ml_dtypes.float8_e4m3fn).astype(np.float64)
    else:
        nib = np.empty((g, 128, n, 4), np.uint8)
        nib[..., 0::2] = words & 0xF
        nib[..., 1::2] = words >> 4
        vals = E2M1[nib]
    vals = vals * np.repeat(np.exp2(scales.astype(np.float64) - 127.0), 8, axis=1)[..., None]
    return vals.transpose(0, 1, 3, 2).reshape(g * 512, n)


def gelu(v):
    return 0.5 * v * (1.0 + np.tanh(np.sqrt(2.0 / np.pi) * (v + 0.044715 * v**3)))


def striped8(idx):
    return np.concatenate([v.reshape(-1, 16).T for v in idx]).astype(np.uint16)


def unstriped8(offs):
    return np.stack([offs[16 * g:16 * g + 16].T.reshape(-1) for g in range(8)]).astype(np.int64)


def put_heads(h, wgs, idx8, t2):
    r = np.arange(h.shape[0])
    page = np.zeros((h.shape[0], t2))
    page[r[:, None], idx8[r % 512 // 64]] = wgs[r // 4 % 128] * h
    return page


K, T, H, S, T2, P, N = 1024, 2048, 1024, 512, 1024, 512, 512


def setup_inputs():
    n = np.random.standard_normal
    s = mx_kscale(K)[:, None]
    u = mx_kscale(H)[:, None]
    tab_words, tab_scales = pack_weight(n((K, T)) * s, "e4m3")
    w1 = (n((K, H)) / np.sqrt(K) / s * u.T).astype(np.float32)
    w2_words, w2_scales = pack_weight(n((K, H)) / np.sqrt(K) / s * u.T, "e2m1")
    w3 = (0.55 * n((K, H)) / np.sqrt(K) / s).astype(np.float32)
    w4_words, w4_scales = pack_weight(n((H, N)) / np.sqrt(H) / u, "e4m3")
    return {
        "tab_words": tab_words, "tab_scales": tab_scales,
        "offs": striped(np.random.permutation(T)[:S]),
        "offs2": striped8(np.stack([np.random.permutation(T2)[:S] for _ in range(8)])),
        "offs3": striped(np.random.permutation(T2)[:P]),
        "w1": w1, "w2_words": w2_words, "w2_scales": w2_scales, "w3": w3,
        "wgs": np.repeat(np.random.uniform(0.5, 2.0, (8, S)), 16, axis=0).astype(np.float32),
        "slotgain": np.exp(0.3 * n(H)).astype(np.float32),
        "site": (0.7 * n((H, P)) * u).astype(np.float32),
        "w4_words": w4_words, "w4_scales": w4_scales,
        "bias": (0.5 * n(N)).astype(np.float32),
    }


def reference(tab_words, tab_scales, offs, offs2, offs3, w1, w2_words, w2_scales, w3, wgs, slotgain, site, w4_words, w4_scales, bias):
    v = unpack_weight(tab_words, tab_scales, "e4m3")[:, unstriped(offs)]
    left = mxq(f64(w1), 0, "e4m3").T @ v
    right = unpack_weight(w2_words, w2_scales, "e2m1").T @ v
    phase = mxq(f64(w3), 0, "e4m3").T @ v
    h = np.maximum(left, right) * np.cos(phase)
    page = put_heads(h, f64(wgs), unstriped8(offs2), T2)
    x = page[:, unstriped(offs3)]
    z = f64(slotgain)[:, None] * x + f64(site)
    zq = mxq(z, 0, "e4m3")
    y = unpack_weight(w4_words, w4_scales, "e4m3").T @ zq
    return np.abs(y + f64(bias)[:, None])

@@ -1,0 +1,275 @@
+import math
+from contextlib import ExitStack
+
+import concourse.mybir as mybir
+
+K, T, H, S, T2, M, N = 1024, 2048, 1024, 512, 1024, 512, 512
+FLOPS = 2 * (3 * K * H * S + H * N * M)
+
+F32 = mybir.dt.float32
+BF16 = mybir.dt.bfloat16
+I32 = mybir.dt.int32
+U32 = mybir.dt.uint32
+U16 = mybir.dt.uint16
+U8 = mybir.dt.uint8
+FP8X4 = mybir.dt.float8_e4m3fn_x4
+FP4X4 = mybir.dt.float4_e2m1fn_x4
+ALU = mybir.AluOpType
+ACT = mybir.ActivationFunctionType
+
+P = 128
+PACK = 4
+PASS = P * PACK
+K_PASSES = K // PASS
+R_PASSES = H // PASS
+SLICES = R_PASSES * PACK
+HALF = M // 2
+
+
+def tile_list_bearing_slot_scorer_kernel(
+    tc, tab_words, tab_scales, offs, offs2, offs3, w1, w2_words, w2_scales, w3, wgs, slotgain, site,
+    w4_words, w4_scales, bias, out,
+):
+    nc = tc.nc
+    with ExitStack() as ctx:
+        keep = ctx.enter_context(tc.tile_pool(name="keep", bufs=1))
+        work = ctx.enter_context(tc.tile_pool(name="work", bufs=1))
+        psum = ctx.enter_context(tc.psum_pool(name="psum", bufs=1))
+
+        list1 = keep.tile([P, S // 16], U16, name="list1")
+        list2 = keep.tile([P, S // 16], U16, name="list2")
+        list3 = keep.tile([P, M // 16], U16, name="list3")
+
+        tab_w = [keep.tile([P, T], U32, name=f"tab_w{a}", align_bytes=64) for a in range(K_PASSES)]
+        tab_s = keep.tile([P, K_PASSES, T], U8, name="tab_s", align_bytes=64)
+        w2_w = keep.tile([P, K_PASSES, 2 * H], U8, name="w2_w", align_bytes=64)
+        w2_s = keep.tile([P, K_PASSES, H], U8, name="w2_s", align_bytes=64)
+        w4_w = keep.tile([P, R_PASSES, N], U32, name="w4_w", align_bytes=64)
+        w4_s = keep.tile([P, R_PASSES, N], U8, name="w4_s", align_bytes=64)
+        wgs_sb = keep.tile([P, S], F32, name="wgs_sb")
+        gain = keep.tile([P, R_PASSES, PACK], F32, name="gain")
+        bias_sb = keep.tile([P, N // P], F32, name="bias_sb")
+        site_sb = [keep.tile([P, PACK, M], F32, name=f"site{b}") for b in range(R_PASSES)]
+        pages = [keep.tile([P, T2], F32, name=f"page{i}") for i in range(2)]
+
+        for plane in (tab_s, w2_s, w4_s):
+            nc.vector.memset(plane[:].bitcast(I32), 0)
+        for page in pages:
+            nc.vector.memset(page[:], 0.0)
+
+        def load_scales(plane, rows):
+            for quad in range(4):
+                nc.sync.dma_start(
+                    out=plane[32 * quad : 32 * quad + 4].bitcast(I32),
+                    in_=rows.bitcast(I32)[:, 4 * quad : 4 * quad + 4, :].rearrange("a r c -> r a c"),
+                )
+
+        raw = {}
+
+        def load_weight(name, w, a, b, c0, c1):
+            tile = work.tile([P, PACK, c1 - c0], F32, name=f"raw_{name}{a}{b}{c0}", tag="raw", bufs=9)
+            rows = w[PASS * a : PASS * (a + 1), PASS * b + c0 : PASS * b + c1]
+            nc.sync.dma_start(out=tile[:], in_=rows.rearrange("(p j) c -> p j c", j=PACK))
+            raw.setdefault((name, a, b), []).append((tile, c0, c1))
+
+        nc.sync.dma_start(list1[:], offs)
+        for a in range(K_PASSES):
+            nc.sync.dma_start(
+                out=tab_w[a][:].bitcast(I32), in_=tab_words[a].rearrange("p t i -> p (t i)").bitcast(I32)
+            )
+        load_scales(tab_s, tab_scales)
+        nc.sync.dma_start(out=w2_w[:].bitcast(I32), in_=w2_words.bitcast(I32).rearrange("a p c -> p a c"))
+        load_weight("w3", w3, 0, 0, 0, PASS)
+        load_weight("w3", w3, 1, 0, 0, PASS)
+        load_scales(w2_s, w2_scales)
+        nc.sync.dma_start(out=gain[:], in_=slotgain.rearrange("(b p t) -> p b t", b=R_PASSES, t=PACK))
+        load_weight("w1", w1, 0, 0, 0, PASS)
+        load_weight("w1", w1, 1, 0, 0, PASS // 2)
+        load_weight("w1", w1, 1, 0, PASS // 2, PASS)
+        nc.sync.dma_start(out=wgs_sb[:], in_=wgs)
+        nc.sync.dma_start(list2[:], offs2)
+        nc.sync.dma_start(list3[:], offs3)
+        nc.sync.dma_start(out=site_sb[0][:], in_=site[0:PASS, :].rearrange("(p t) m -> p t m", t=PACK))
+        for name, w in (("w3", w3), ("w1", w1)):
+            for a in range(K_PASSES):
+                load_weight(name, w, a, 1, 0, PASS)
+        nc.sync.dma_start(out=site_sb[1][:], in_=site[PASS : 2 * PASS, :].rearrange("(p t) m -> p t m", t=PACK))
+        nc.sync.dma_start(
+            out=w4_w[:].bitcast(I32), in_=w4_words.rearrange("b p c i -> p b (c i)").bitcast(I32)
+        )
+        load_scales(w4_s, w4_scales)
+        with nc.allow_non_contiguous_dma(reason="one small vector laid along the partitions"):
+            nc.sync.dma_start(out=bias_sb[:], in_=bias.rearrange("(c p) -> p c", p=P))
+
+        v_w = [keep.tile([P, S], U32, name=f"v_w{a}", align_bytes=64) for a in range(K_PASSES)]
+        v_s = [keep.tile([P, S], U8, name=f"v_s{a}", align_bytes=64) for a in range(K_PASSES)]
+        for a in range(K_PASSES):
+            nc.vector.tensor_copy(v_w[a][:], tab_w[a][:].indirect(list1[:]))
+            nc.vector.tensor_copy(v_s[a][:], tab_s[:, a, :].indirect(list1[:]))
+
+        w2_wd = keep.tile([P, K_PASSES, R_PASSES, PACK, 2 * P], U8, name="w2_wd", align_bytes=64)
+        w2_sd = keep.tile([P, K_PASSES, R_PASSES, PACK, P], U8, name="w2_sd", align_bytes=64)
+        nc.vector.tensor_copy(
+            out=w2_wd[:].bitcast(U16).rearrange("p a b t q -> p (a b) q t"),
+            in_=w2_w[:].bitcast(U16).rearrange("p a (b q t) -> p (a b) q t", b=R_PASSES, t=PACK),
+        )
+        nc.vector.tensor_copy(
+            out=w2_sd[:].rearrange("p a b t q -> p (a b) q t"),
+            in_=w2_s[:].rearrange("p a (b q t) -> p (a b) q t", b=R_PASSES, t=PACK),
+        )
+
+        codes = {}
+
+        def quantise_weight(name, a, b, cast, tag, bufs, cuts):
+            grouped = work.tile([P, PACK, P, PACK], BF16, name=f"grp_{name}{a}{b}", tag=tag, bufs=bufs, align_bytes=64)
+            for tile, c0, c1 in raw[(name, a, b)]:
+                cast(
+                    out=grouped[:, :, c0 // PACK : c1 // PACK, :].rearrange("p t q j -> p q j t"),
+                    in_=tile[:].rearrange("p j (q t) -> p q j t", t=PACK),
+                )
+            words = keep.tile([P, PASS], U32, name=f"words_{name}{a}{b}", align_bytes=64)
+            scales = keep.tile([P, PASS], U8, name=f"scales_{name}{a}{b}", align_bytes=64)
+            for t0, t1 in cuts:
+                nc.vector.quantize_mx(
+                    out=words[:, P * t0 : P * t1].bitcast(FP8X4),
+                    scales=scales[:, P * t0 : P * t1],
+                    in_=grouped[:, t0:t1].rearrange("p t q j -> p (t q j)"),
+                )
+            codes[(name, a, b)] = (words, scales)
+
+        whole = [(0, PACK)]
+        quantise_weight("w3", 0, 0, nc.scalar.copy, "grouped", 3, whole)
+        quantise_weight("w3", 1, 0, nc.scalar.copy, "grouped", 3, whole)
+        quantise_weight("w1", 0, 0, nc.vector.tensor_copy, "grouped", 3, whole)
+        quantise_weight("w1", 1, 0, nc.vector.tensor_copy, "grouped", 3, [(0, 1), (1, PACK)])
+
+        def product(acc, name, b, t):
+            for a in range(K_PASSES):
+                if name == "w2":
+                    lhs, lhs_scale = w2_wd[:, a, b, t, :].bitcast(FP4X4), w2_sd[:, a, b, t, :]
+                else:
+                    words, scales = codes[(name, a, b)]
+                    lhs, lhs_scale = words[:, P * t : P * (t + 1)].bitcast(FP8X4), scales[:, P * t : P * (t + 1)]
+                nc.tensor.matmul_mx(
+                    out=acc[:], lhsT=lhs, lhsT_scale=lhs_scale, rhs=v_w[a][:].bitcast(FP8X4), rhs_scale=v_s[a][:],
+                    start=(a == 0), stop=(a == K_PASSES - 1),
+                )
+
+        larger, cosine, feature = {}, {}, {}
+
+        def readings(s):
+            b, t = divmod(s, PACK)
+            right_ps = psum.tile([P, S], F32, name=f"right_ps{s}", tag="right")
+            product(right_ps, "w2", b, t)
+            right = work.tile([P, S], F32, name=f"right{s}", tag="right", bufs=3)
+            nc.scalar.copy(out=right[:], in_=right_ps[:])
+            phase_ps = psum.tile([P, S], F32, name=f"phase_ps{s}", tag="phase")
+            product(phase_ps, "w3", b, t)
+            size = work.tile([P, S], F32, name=f"size{s}", tag="size", bufs=2)
+            nc.scalar.activation(out=size[:], in_=phase_ps[:], func=ACT.Abs)
+            cosine[s] = work.tile([P, S], F32, name=f"cosine{s}", tag="cosine", bufs=3)
+            nc.scalar.activation(out=cosine[s][:], in_=size[:], func=ACT.Sin, scale=-1.0, bias=math.pi / 2)
+            left_ps = psum.tile([P, S], F32, name=f"left_ps{s}", tag="left", bufs=2)
+            product(left_ps, "w1", b, t)
+            larger[s] = work.tile([P, S], F32, name=f"larger{s}", tag="larger", bufs=2)
+            nc.vector.tensor_tensor(out=larger[s][:], in0=left_ps[:], in1=right[:], op=ALU.max)
+
+        def make_feature(s, tag, bufs):
+            b, t = divmod(s, PACK)
+            feature[s] = work.tile([P, S], F32, name=f"feature{s}", tag=tag, bufs=bufs, align_bytes=64)
+            nc.vector.scalar_tensor_tensor(
+                out=feature[s][:], in0=larger[s][:], scalar=gain[:, b, t : t + 1], in1=cosine[s][:],
+                op0=ALU.mult, op1=ALU.mult,
+            )
+
+        def place(s):
+            nc.vector.tensor_tensor(pages[s % 2][:].indirect(list2[:]), feature[s][:], wgs_sb[:], ALU.mult)
+
+        z_f32 = {}
+
+        def fetch(s, m0, m1):
+            b, t = divmod(s, PACK)
+            if b not in z_f32:
+                z_f32[b] = work.tile([P, PACK, M], F32, name=f"z_f32_{b}", tag="raw", bufs=9)
+            nc.vector.tensor_tensor(
+                z_f32[b][:, t, m0:m1], pages[s % 2][:].indirect(list3[:, m0 // 16 : m1 // 16]),
+                site_sb[b][:, t, m0:m1], ALU.add,
+            )
+
+        z_bf16 = [keep.tile([P, M, PACK], BF16, name=f"z_bf16_{b}", align_bytes=64) for b in range(R_PASSES)]
+        z_w = [keep.tile([P, M], U32, name=f"z_w{b}", align_bytes=64) for b in range(R_PASSES)]
+        z_s = [keep.tile([P, M], U8, name=f"z_s{b}", align_bytes=64) for b in range(R_PASSES)]
+
+        def round_z(b, m0, m1, cast):
+            cast(
+                out=z_bf16[b][:, m0:m1, :].rearrange("p (c i) t -> p c t i", i=4),
+                in_=z_f32[b][:, :, m0:m1].rearrange("p t (c i) -> p c t i", i=4),
+            )
+
+        def quantise_z(b, m0, m1):
+            nc.vector.quantize_mx(
+                out=z_w[b][:, m0:m1].bitcast(FP8X4), scales=z_s[b][:, m0:m1],
+                in_=z_bf16[b][:, m0:m1, :].rearrange("p m t -> p (m t)"),
+            )
+
+        score_ps = {
+            (half, pair): psum.tile([P, 2, HALF], F32, name=f"score_ps{half}{pair}")
+            for half in range(2) for pair in range(2)
+        }
+
+        def score_passes(b, half):
+            cols = slice(HALF * half, HALF * (half + 1))
+            for pair in range(2):
+                for i in range(2):
+                    rows = slice(P * (2 * pair + i), P * (2 * pair + i + 1))
+                    nc.tensor.matmul_mx(
+                        out=score_ps[(half, pair)][:, i, :],
+                        lhsT=w4_w[:, b, rows].bitcast(FP8X4), lhsT_scale=w4_s[:, b, rows],
+                        rhs=z_w[b][:, cols].bitcast(FP8X4), rhs_scale=z_s[b][:, cols],
+                        start=(b == 0 and i == 0), stop=(b == R_PASSES - 1 and i == 1),
+                    )
+
+        def store_scores(half):
+            for pair in range(2):
+                score = work.tile([P, 2, HALF], F32, name=f"score{half}{pair}", tag="score", bufs=4)
+                for i in range(2):
+                    c = 2 * pair + i
+                    nc.scalar.activation(
+                        out=score[:, i, :], in_=score_ps[(half, pair)][:, i, :], func=ACT.Abs, bias=bias_sb[:, c : c + 1]
+                    )
+                rows = out[2 * P * pair : 2 * P * (pair + 1), HALF * half : HALF * (half + 1)]
+                nc.sync.dma_start(out=rows.rearrange("(i p) m -> p i m", p=P), in_=score[:])
+
+        readings(0)
+        make_feature(0, "feature", 2)
+        readings(1)
+        last = SLICES - 1
+        for s in range(SLICES):
+            place(s)
+            if s == 1:
+                quantise_weight("w3", 0, 1, nc.scalar.copy, "grouped", 3, whole)
+                quantise_weight("w3", 1, 1, nc.scalar.copy, "grouped", 3, whole)
+            if s == 2:
+                quantise_weight("w1", 0, 1, nc.scalar.copy, "grouped", 3, whole)
+                quantise_weight("w1", 1, 1, nc.scalar.copy, "held", 1, whole)
+                make_feature(s + 1, "held", 1)
+            elif s < last:
+                make_feature(s + 1, "feature", 2)
+            if s == PACK + 1:
+                quantise_z(0, 0, M)
+                score_passes(0, 0)
+                score_passes(0, 1)
+            if s < last:
+                fetch(s, 0, M)
+            if s + 2 < SLICES:
+                readings(s + 2)
+            if s == PACK - 1:
+                round_z(0, 0, M, nc.scalar.copy)
+        fetch(last, 0, HALF)
+        round_z(1, 0, HALF, nc.scalar.copy)
+        fetch(last, HALF, M)
+        round_z(1, HALF, M, nc.vector.tensor_copy)
+        for half in range(2):
+            quantise_z(1, HALF * half, HALF * (half + 1))
+            score_passes(1, half)
+            store_scores(half)

@@ -23,7 +23,9 @@ PASS = P * PACK
 K_PASSES = K // PASS
 R_PASSES = H // PASS
 SLICES = R_PASSES * PACK
-HALF = M // 2
+PIECES = 4
+PIECE = M // PIECES
+N_TILES = N // P
 
 
 def tile_list_bearing_slot_scorer_kernel(
@@ -42,7 +44,7 @@ def tile_list_bearing_slot_scorer_kernel(
 
         tab_w = [keep.tile([P, T], U32, name=f"tab_w{a}", align_bytes=64) for a in range(K_PASSES)]
         tab_s = keep.tile([P, K_PASSES, T], U8, name="tab_s", align_bytes=64)
-        w2_w = keep.tile([P, K_PASSES, 2 * H], U8, name="w2_w", align_bytes=64)
+        w2_w = [keep.tile([P, 2 * H], U8, name=f"w2_w{a}", align_bytes=64) for a in range(K_PASSES)]
         w2_s = keep.tile([P, K_PASSES, H], U8, name="w2_s", align_bytes=64)
         w4_w = keep.tile([P, R_PASSES, N], U32, name="w4_w", align_bytes=64)
         w4_s = keep.tile([P, R_PASSES, N], U8, name="w4_s", align_bytes=64)
@@ -52,43 +54,53 @@ def tile_list_bearing_slot_scorer_kernel(
         site_sb = [keep.tile([P, PACK, M], F32, name=f"site{b}") for b in range(R_PASSES)]
         pages = [keep.tile([P, T2], F32, name=f"page{i}") for i in range(2)]
 
+        warm = keep.tile([P, 2], F32, name="warm")
+        nc.vector.memset(warm[:], 0.0)
+        nc.scalar.activation(out=warm[:, 1:2], in_=warm[:, 0:1], func=ACT.Sin)
         for plane in (tab_s, w2_s, w4_s):
             nc.vector.memset(plane[:].bitcast(I32), 0)
         for page in pages:
             nc.vector.memset(page[:], 0.0)
 
-        def load_scales(plane, rows):
-            for quad in range(4):
-                nc.sync.dma_start(
-                    out=plane[32 * quad : 32 * quad + 4].bitcast(I32),
-                    in_=rows.bitcast(I32)[:, 4 * quad : 4 * quad + 4, :].rearrange("a r c -> r a c"),
+        def load_scales(queue, plane, rows):
+            for r in range(4):
+                queue.dma_start(
+                    out=plane[r:P:32].bitcast(I32),
+                    in_=rows.bitcast(I32)[:, r:16:4, :].rearrange("a q c -> q a c"),
                 )
 
         raw = {}
 
         def load_weight(name, w, a, b, c0, c1):
-            tile = work.tile([P, PACK, c1 - c0], F32, name=f"raw_{name}{a}{b}{c0}", tag="raw", bufs=9)
+            tile = work.tile([P, PACK, c1 - c0], F32, name=f"raw_{name}{a}{b}{c0}", tag=f"raw{c1 - c0}", bufs=7 if c1 - c0 == PASS else 2)
             rows = w[PASS * a : PASS * (a + 1), PASS * b + c0 : PASS * b + c1]
             nc.sync.dma_start(out=tile[:], in_=rows.rearrange("(p j) c -> p j c", j=PACK))
             raw.setdefault((name, a, b), []).append((tile, c0, c1))
 
-        nc.sync.dma_start(list1[:], offs)
-        for a in range(K_PASSES):
+        def load_table(a):
             nc.sync.dma_start(
                 out=tab_w[a][:].bitcast(I32), in_=tab_words[a].rearrange("p t i -> p (t i)").bitcast(I32)
             )
-        load_scales(tab_s, tab_scales)
-        nc.sync.dma_start(out=w2_w[:].bitcast(I32), in_=w2_words.bitcast(I32).rearrange("a p c -> p a c"))
-        load_weight("w3", w3, 0, 0, 0, PASS)
-        load_weight("w3", w3, 1, 0, 0, PASS)
-        load_scales(w2_s, w2_scales)
+
+        def load_w2(a):
+            nc.sync.dma_start(out=w2_w[a][:].bitcast(I32), in_=w2_words[a].bitcast(I32))
+
+        nc.sync.dma_start(list1[:], offs)
+        load_w2(0)
+        nc.sync.dma_start(list2[:], offs2)
+        nc.sync.dma_start(list3[:], offs3)
         nc.sync.dma_start(out=gain[:], in_=slotgain.rearrange("(b p t) -> p b t", b=R_PASSES, t=PACK))
+        load_w2(1)
+        load_table(0)
+        load_table(1)
+        load_scales(nc.sync, tab_s, tab_scales)
+        load_weight("w3", w3, 0, 0, 0, PASS)
+        load_scales(nc.sync, w2_s, w2_scales)
+        load_weight("w3", w3, 1, 0, 0, PASS)
         load_weight("w1", w1, 0, 0, 0, PASS)
         load_weight("w1", w1, 1, 0, 0, PASS // 2)
         load_weight("w1", w1, 1, 0, PASS // 2, PASS)
         nc.sync.dma_start(out=wgs_sb[:], in_=wgs)
-        nc.sync.dma_start(list2[:], offs2)
-        nc.sync.dma_start(list3[:], offs3)
         nc.sync.dma_start(out=site_sb[0][:], in_=site[0:PASS, :].rearrange("(p t) m -> p t m", t=PACK))
         for name, w in (("w3", w3), ("w1", w1)):
             for a in range(K_PASSES):
@@ -97,22 +109,24 @@ def tile_list_bearing_slot_scorer_kernel(
         nc.sync.dma_start(
             out=w4_w[:].bitcast(I32), in_=w4_words.rearrange("b p c i -> p b (c i)").bitcast(I32)
         )
-        load_scales(w4_s, w4_scales)
+        load_scales(nc.sync, w4_s, w4_scales)
         with nc.allow_non_contiguous_dma(reason="one small vector laid along the partitions"):
             nc.sync.dma_start(out=bias_sb[:], in_=bias.rearrange("(c p) -> p c", p=P))
 
         v_w = [keep.tile([P, S], U32, name=f"v_w{a}", align_bytes=64) for a in range(K_PASSES)]
         v_s = [keep.tile([P, S], U8, name=f"v_s{a}", align_bytes=64) for a in range(K_PASSES)]
-        for a in range(K_PASSES):
-            nc.vector.tensor_copy(v_w[a][:], tab_w[a][:].indirect(list1[:]))
-            nc.vector.tensor_copy(v_s[a][:], tab_s[:, a, :].indirect(list1[:]))
 
         w2_wd = keep.tile([P, K_PASSES, R_PASSES, PACK, 2 * P], U8, name="w2_wd", align_bytes=64)
         w2_sd = keep.tile([P, K_PASSES, R_PASSES, PACK, P], U8, name="w2_sd", align_bytes=64)
-        nc.vector.tensor_copy(
-            out=w2_wd[:].bitcast(U16).rearrange("p a b t q -> p (a b) q t"),
-            in_=w2_w[:].bitcast(U16).rearrange("p a (b q t) -> p (a b) q t", b=R_PASSES, t=PACK),
-        )
+        for a in range(K_PASSES):
+            nc.vector.tensor_copy(
+                out=w2_wd[:, a].bitcast(U16).rearrange("p b t q -> p b q t"),
+                in_=w2_w[a][:].bitcast(U16).rearrange("p (b q t) -> p b q t", b=R_PASSES, t=PACK),
+            )
+        for a in range(K_PASSES):
+            nc.vector.tensor_copy(v_w[a][:], tab_w[a][:].indirect(list1[:]))
+        for a in range(K_PASSES):
+            nc.vector.tensor_copy(v_s[a][:], tab_s[:, a, :].indirect(list1[:]))
         nc.vector.tensor_copy(
             out=w2_sd[:].rearrange("p a b t q -> p (a b) q t"),
             in_=w2_s[:].rearrange("p a (b q t) -> p (a b) q t", b=R_PASSES, t=PACK),
@@ -120,13 +134,15 @@ def tile_list_bearing_slot_scorer_kernel(
 
         codes = {}
 
-        def quantise_weight(name, a, b, cast, tag, bufs, cuts):
+        def quantise_weight(name, a, b, split, tag, bufs, cuts):
             grouped = work.tile([P, PACK, P, PACK], BF16, name=f"grp_{name}{a}{b}", tag=tag, bufs=bufs, align_bytes=64)
             for tile, c0, c1 in raw[(name, a, b)]:
-                cast(
-                    out=grouped[:, :, c0 // PACK : c1 // PACK, :].rearrange("p t q j -> p q j t"),
-                    in_=tile[:].rearrange("p j (q t) -> p q j t", t=PACK),
-                )
+                for cast, lo, hi in ((nc.scalar.copy, c0, min(c1, split)), (nc.vector.tensor_copy, max(c0, split), c1)):
+                    if lo < hi:
+                        cast(
+                            out=grouped[:, :, lo // PACK : hi // PACK, :].rearrange("p t q j -> p q j t"),
+                            in_=tile[:, :, lo - c0 : hi - c0].rearrange("p j (q t) -> p q j t", t=PACK),
+                        )
             words = keep.tile([P, PASS], U32, name=f"words_{name}{a}{b}", align_bytes=64)
             scales = keep.tile([P, PASS], U8, name=f"scales_{name}{a}{b}", align_bytes=64)
             for t0, t1 in cuts:
@@ -138,10 +154,10 @@ def tile_list_bearing_slot_scorer_kernel(
             codes[(name, a, b)] = (words, scales)
 
         whole = [(0, PACK)]
-        quantise_weight("w3", 0, 0, nc.scalar.copy, "grouped", 3, whole)
-        quantise_weight("w3", 1, 0, nc.scalar.copy, "grouped", 3, whole)
-        quantise_weight("w1", 0, 0, nc.vector.tensor_copy, "grouped", 3, whole)
-        quantise_weight("w1", 1, 0, nc.vector.tensor_copy, "grouped", 3, [(0, 1), (1, PACK)])
+        quantise_weight("w3", 0, 0, PASS, "stage_c", 1, whole)
+        quantise_weight("w3", 1, 0, 192, "stage_b", 1, whole)
+        quantise_weight("w1", 0, 0, PASS // 2, "stage_a", 1, whole)
+        quantise_weight("w1", 1, 0, 0, "stage_d", 1, [(0, 1), (1, PACK)])
 
         def product(acc, name, b, t):
             for a in range(K_PASSES):
@@ -157,21 +173,25 @@ def tile_list_bearing_slot_scorer_kernel(
 
         larger, cosine, feature = {}, {}, {}
 
+        def slice_tile(kind, s, bufs, first_tag):
+            tag, depth = (first_tag, 1) if s == 0 else (kind, bufs)
+            return work.tile([P, S], F32, name=f"{kind}{s}", tag=tag, bufs=depth, align_bytes=64)
+
         def readings(s):
             b, t = divmod(s, PACK)
             right_ps = psum.tile([P, S], F32, name=f"right_ps{s}", tag="right")
             product(right_ps, "w2", b, t)
-            right = work.tile([P, S], F32, name=f"right{s}", tag="right", bufs=3)
+            right = slice_tile("right", s, 3, "stage_a")
             nc.scalar.copy(out=right[:], in_=right_ps[:])
             phase_ps = psum.tile([P, S], F32, name=f"phase_ps{s}", tag="phase")
             product(phase_ps, "w3", b, t)
             size = work.tile([P, S], F32, name=f"size{s}", tag="size", bufs=2)
             nc.scalar.activation(out=size[:], in_=phase_ps[:], func=ACT.Abs)
-            cosine[s] = work.tile([P, S], F32, name=f"cosine{s}", tag="cosine", bufs=3)
+            cosine[s] = slice_tile("cosine", s, 3, "stage_c")
             nc.scalar.activation(out=cosine[s][:], in_=size[:], func=ACT.Sin, scale=-1.0, bias=math.pi / 2)
             left_ps = psum.tile([P, S], F32, name=f"left_ps{s}", tag="left", bufs=2)
             product(left_ps, "w1", b, t)
-            larger[s] = work.tile([P, S], F32, name=f"larger{s}", tag="larger", bufs=2)
+            larger[s] = slice_tile("larger", s, 2, "stage_b")
             nc.vector.tensor_tensor(out=larger[s][:], in0=left_ps[:], in1=right[:], op=ALU.max)
 
         def make_feature(s, tag, bufs):
@@ -190,86 +210,98 @@ def tile_list_bearing_slot_scorer_kernel(
         def fetch(s, m0, m1):
             b, t = divmod(s, PACK)
             if b not in z_f32:
-                z_f32[b] = work.tile([P, PACK, M], F32, name=f"z_f32_{b}", tag="raw", bufs=9)
+                z_f32[b] = keep.tile([P, PACK, M], F32, name=f"z_f32_{b}")
             nc.vector.tensor_tensor(
                 z_f32[b][:, t, m0:m1], pages[s % 2][:].indirect(list3[:, m0 // 16 : m1 // 16]),
                 site_sb[b][:, t, m0:m1], ALU.add,
             )
 
-        z_bf16 = [keep.tile([P, M, PACK], BF16, name=f"z_bf16_{b}", align_bytes=64) for b in range(R_PASSES)]
+        z_bf16 = {}
         z_w = [keep.tile([P, M], U32, name=f"z_w{b}", align_bytes=64) for b in range(R_PASSES)]
         z_s = [keep.tile([P, M], U8, name=f"z_s{b}", align_bytes=64) for b in range(R_PASSES)]
 
         def round_z(b, m0, m1, cast):
+            z_bf16[(b, m0)] = keep.tile([P, m1 - m0, PACK], BF16, name=f"z_bf16_{b}_{m0}", align_bytes=64)
             cast(
-                out=z_bf16[b][:, m0:m1, :].rearrange("p (c i) t -> p c t i", i=4),
+                out=z_bf16[(b, m0)][:].rearrange("p (c i) t -> p c t i", i=4),
                 in_=z_f32[b][:, :, m0:m1].rearrange("p t (c i) -> p c t i", i=4),
             )
 
         def quantise_z(b, m0, m1):
             nc.vector.quantize_mx(
                 out=z_w[b][:, m0:m1].bitcast(FP8X4), scales=z_s[b][:, m0:m1],
-                in_=z_bf16[b][:, m0:m1, :].rearrange("p m t -> p (m t)"),
+                in_=z_bf16[(b, m0)][:].rearrange("p m t -> p (m t)"),
             )
 
-        score_ps = {
-            (half, pair): psum.tile([P, 2, HALF], F32, name=f"score_ps{half}{pair}")
-            for half in range(2) for pair in range(2)
-        }
+        score_ps = [psum.tile([P, N_TILES, PIECE], F32, name=f"score_ps{u}") for u in range(PIECES)]
 
-        def score_passes(b, half):
-            cols = slice(HALF * half, HALF * (half + 1))
-            for pair in range(2):
-                for i in range(2):
-                    rows = slice(P * (2 * pair + i), P * (2 * pair + i + 1))
-                    nc.tensor.matmul_mx(
-                        out=score_ps[(half, pair)][:, i, :],
-                        lhsT=w4_w[:, b, rows].bitcast(FP8X4), lhsT_scale=w4_s[:, b, rows],
-                        rhs=z_w[b][:, cols].bitcast(FP8X4), rhs_scale=z_s[b][:, cols],
-                        start=(b == 0 and i == 0), stop=(b == R_PASSES - 1 and i == 1),
-                    )
+        def score_passes(b, u):
+            cols = slice(PIECE * u, PIECE * (u + 1))
+            for c in range(N_TILES):
+                rows = slice(P * c, P * (c + 1))
+                nc.tensor.matmul_mx(
+                    out=score_ps[u][:, c, :],
+                    lhsT=w4_w[:, b, rows].bitcast(FP8X4), lhsT_scale=w4_s[:, b, rows],
+                    rhs=z_w[b][:, cols].bitcast(FP8X4), rhs_scale=z_s[b][:, cols],
+                    start=(b == 0 and c == 0), stop=(b == R_PASSES - 1 and c == N_TILES - 1),
+                )
 
-        def store_scores(half):
-            for pair in range(2):
-                score = work.tile([P, 2, HALF], F32, name=f"score{half}{pair}", tag="score", bufs=4)
-                for i in range(2):
-                    c = 2 * pair + i
+        def store_scores(u):
+            score = work.tile([P, N_TILES, PIECE], F32, name=f"score{u}", tag="score", bufs=PIECES)
+            if u == PIECES - 2:
+                signed = work.tile([P, N_TILES, PIECE], F32, name="signed", tag="larger", bufs=2, align_bytes=64)
+                nc.vector.tensor_tensor(
+                    out=signed[:], in0=score_ps[u][:], in1=bias_sb[:].unsqueeze(2).to_broadcast([P, N_TILES, PIECE]),
+                    op=ALU.add,
+                )
+                nc.vector.scalar_tensor_tensor(
+                    out=score[:], in0=signed[:], scalar=-1.0, in1=signed[:], op0=ALU.mult, op1=ALU.max
+                )
+            else:
+                for c in range(N_TILES):
                     nc.scalar.activation(
-                        out=score[:, i, :], in_=score_ps[(half, pair)][:, i, :], func=ACT.Abs, bias=bias_sb[:, c : c + 1]
+                        out=score[:, c, :], in_=score_ps[u][:, c, :], func=ACT.Abs, bias=bias_sb[:, c : c + 1]
                     )
-                rows = out[2 * P * pair : 2 * P * (pair + 1), HALF * half : HALF * (half + 1)]
-                nc.sync.dma_start(out=rows.rearrange("(i p) m -> p i m", p=P), in_=score[:])
+            cols = out[:, PIECE * u : PIECE * (u + 1)]
+            nc.sync.dma_start(out=cols.rearrange("(c p) m -> p c m", p=P), in_=score[:])
 
         readings(0)
-        make_feature(0, "feature", 2)
+        make_feature(0, "stage_d", 1)
         readings(1)
         last = SLICES - 1
         for s in range(SLICES):
             place(s)
             if s == 1:
-                quantise_weight("w3", 0, 1, nc.scalar.copy, "grouped", 3, whole)
-                quantise_weight("w3", 1, 1, nc.scalar.copy, "grouped", 3, whole)
+                quantise_weight("w3", 0, 1, PASS, "stage_a", 1, whole)
+                quantise_weight("w3", 1, 1, PASS, "stage_b", 1, whole)
             if s == 2:
-                quantise_weight("w1", 0, 1, nc.scalar.copy, "grouped", 3, whole)
-                quantise_weight("w1", 1, 1, nc.scalar.copy, "held", 1, whole)
-                make_feature(s + 1, "held", 1)
+                quantise_weight("w1", 0, 1, PASS, "stage_c", 1, whole)
+                quantise_weight("w1", 1, 1, PASS, "stage_d", 1, whole)
+                make_feature(s + 1, "stage_d", 1)
             elif s < last:
                 make_feature(s + 1, "feature", 2)
             if s == PACK + 1:
                 quantise_z(0, 0, M)
-                score_passes(0, 0)
-                score_passes(0, 1)
+                for u in range(PIECES):
+                    score_passes(0, u)
             if s < last:
                 fetch(s, 0, M)
             if s + 2 < SLICES:
                 readings(s + 2)
             if s == PACK - 1:
                 round_z(0, 0, M, nc.scalar.copy)
-        fetch(last, 0, HALF)
-        round_z(1, 0, HALF, nc.scalar.copy)
-        fetch(last, HALF, M)
-        round_z(1, HALF, M, nc.vector.tensor_copy)
-        for half in range(2):
-            quantise_z(1, HALF * half, HALF * (half + 1))
-            score_passes(1, half)
-            store_scores(half)
+        def piece(u):
+            return PIECE * u, PIECE * (u + 1)
+
+        for step in range(PIECES + 2):
+            if step < PIECES:
+                fetch(last, *piece(step))
+                if step % 2 == 1:
+                    round_z(1, *piece(step), nc.scalar.copy)
+            if step % 2 == 1 and step - 1 < PIECES:
+                round_z(1, *piece(step - 1), nc.vector.tensor_copy)
+            if step >= 2:
+                quantise_z(1, *piece(step - 2))
+                score_passes(1, step - 2)
+        for u in range(PIECES):
+            store_scores(u)

@@ -120,16 +120,16 @@ def tile_list_bearing_slot_scorer_kernel(
         w2_sd = keep.tile([P, K_PASSES, R_PASSES, PACK, P], U8, name="w2_sd", align_bytes=64)
         for a in range(K_PASSES):
             nc.vector.tensor_copy(
-                out=w2_wd[:, a].bitcast(U16).rearrange("p b t q -> p b q t"),
-                in_=w2_w[a][:].bitcast(U16).rearrange("p (b q t) -> p b q t", b=R_PASSES, t=PACK),
+                out=w2_wd[:, a].bitcast(U16).rearrange("p b (u e) q -> p b u q e", e=2),
+                in_=w2_w[a][:].bitcast(U16).rearrange("p (b q u e) -> p b u q e", b=R_PASSES, u=2, e=2),
             )
         for a in range(K_PASSES):
             nc.vector.tensor_copy(v_w[a][:], tab_w[a][:].indirect(list1[:]))
         for a in range(K_PASSES):
             nc.vector.tensor_copy(v_s[a][:], tab_s[:, a, :].indirect(list1[:]))
         nc.vector.tensor_copy(
-            out=w2_sd[:].rearrange("p a b t q -> p (a b) q t"),
-            in_=w2_s[:].rearrange("p a (b q t) -> p (a b) q t", b=R_PASSES, t=PACK),
+            out=w2_sd[:].rearrange("p a b (u e) q -> p (a b) u q e", e=2),
+            in_=w2_s[:].rearrange("p a (b q u e) -> p (a b) u q e", b=R_PASSES, u=2, e=2),
         )
 
         codes = {}
@@ -140,8 +140,8 @@ def tile_list_bearing_slot_scorer_kernel(
                 for cast, lo, hi in ((nc.scalar.copy, c0, min(c1, split)), (nc.vector.tensor_copy, max(c0, split), c1)):
                     if lo < hi:
                         cast(
-                            out=grouped[:, :, lo // PACK : hi // PACK, :].rearrange("p t q j -> p q j t"),
-                            in_=tile[:, :, lo - c0 : hi - c0].rearrange("p j (q t) -> p q j t", t=PACK),
+                            out=grouped[:, :, lo // PACK : hi // PACK, :].rearrange("p (u e) q j -> p u q j e", e=2),
+                            in_=tile[:, :, lo - c0 : hi - c0].rearrange("p j (q u e) -> p u q j e", u=2, e=2),
                         )
             words = keep.tile([P, PASS], U32, name=f"words_{name}{a}{b}", align_bytes=64)
             scales = keep.tile([P, PASS], U8, name=f"scales_{name}{a}{b}", align_bytes=64)
@@ -173,37 +173,49 @@ def tile_list_bearing_slot_scorer_kernel(
 
         larger, cosine, feature = {}, {}, {}
 
-        def slice_tile(kind, s, bufs, first_tag):
-            tag, depth = (first_tag, 1) if s == 0 else (kind, bufs)
+        shared = {
+            ("right", 0): "stage_a", ("larger", 0): "stage_b", ("larger", 1): "stage_c", ("feature", 0): "stage_d",
+            ("feature", PACK - 1): "stage_d",
+        }
+
+        def slice_tile(kind, s, bufs):
+            tag, depth = (shared[(kind, s)], 1) if (kind, s) in shared else (kind, bufs)
             return work.tile([P, S], F32, name=f"{kind}{s}", tag=tag, bufs=depth, align_bytes=64)
 
         def readings(s):
             b, t = divmod(s, PACK)
             right_ps = psum.tile([P, S], F32, name=f"right_ps{s}", tag="right")
             product(right_ps, "w2", b, t)
-            right = slice_tile("right", s, 3, "stage_a")
+            right = slice_tile("right", s, 3)
             nc.scalar.copy(out=right[:], in_=right_ps[:])
             phase_ps = psum.tile([P, S], F32, name=f"phase_ps{s}", tag="phase")
             product(phase_ps, "w3", b, t)
             size = work.tile([P, S], F32, name=f"size{s}", tag="size", bufs=2)
             nc.scalar.activation(out=size[:], in_=phase_ps[:], func=ACT.Abs)
-            cosine[s] = slice_tile("cosine", s, 3, "stage_c")
+            cosine[s] = slice_tile("cosine", s, 3)
             nc.scalar.activation(out=cosine[s][:], in_=size[:], func=ACT.Sin, scale=-1.0, bias=math.pi / 2)
             left_ps = psum.tile([P, S], F32, name=f"left_ps{s}", tag="left", bufs=2)
             product(left_ps, "w1", b, t)
-            larger[s] = slice_tile("larger", s, 2, "stage_b")
+            larger[s] = slice_tile("larger", s, 2)
             nc.vector.tensor_tensor(out=larger[s][:], in0=left_ps[:], in1=right[:], op=ALU.max)
 
-        def make_feature(s, tag, bufs):
+        def make_feature(s):
             b, t = divmod(s, PACK)
-            feature[s] = work.tile([P, S], F32, name=f"feature{s}", tag=tag, bufs=bufs, align_bytes=64)
-            nc.vector.scalar_tensor_tensor(
-                out=feature[s][:], in0=larger[s][:], scalar=gain[:, b, t : t + 1], in1=cosine[s][:],
-                op0=ALU.mult, op1=ALU.mult,
-            )
+            factor = slice_tile("factor", s, 1)
+            feature[s] = slice_tile("feature", s, 2)
+            if s == 0:
+                nc.vector.scalar_tensor_tensor(
+                    out=factor[:], in0=cosine[s][:], scalar=gain[:, b, t : t + 1], in1=wgs_sb[:],
+                    op0=ALU.mult, op1=ALU.mult,
+                )
+                nc.vector.tensor_tensor(out=feature[s][:], in0=larger[s][:], in1=factor[:], op=ALU.mult)
+            else:
+                nc.scalar.activation(out=cosine[s][:], in_=cosine[s][:], func=ACT.Copy, scale=gain[:, b, t : t + 1])
+                nc.gpsimd.tensor_tensor(out=factor[:], in0=cosine[s][:], in1=wgs_sb[:], op=ALU.mult)
+                nc.gpsimd.tensor_tensor(out=feature[s][:], in0=larger[s][:], in1=factor[:], op=ALU.mult)
 
         def place(s):
-            nc.vector.tensor_tensor(pages[s % 2][:].indirect(list2[:]), feature[s][:], wgs_sb[:], ALU.mult)
+            nc.vector.tensor_copy(pages[s % 2][:].indirect(list2[:]), feature[s][:])
 
         z_f32 = {}
 
@@ -266,7 +278,7 @@ def tile_list_bearing_slot_scorer_kernel(
             nc.sync.dma_start(out=cols.rearrange("(c p) m -> p c m", p=P), in_=score[:])
 
         readings(0)
-        make_feature(0, "stage_d", 1)
+        make_feature(0)
         readings(1)
         last = SLICES - 1
         for s in range(SLICES):
@@ -277,9 +289,8 @@ def tile_list_bearing_slot_scorer_kernel(
             if s == 2:
                 quantise_weight("w1", 0, 1, PASS, "stage_c", 1, whole)
                 quantise_weight("w1", 1, 1, PASS, "stage_d", 1, whole)
-                make_feature(s + 1, "stage_d", 1)
-            elif s < last:
-                make_feature(s + 1, "feature", 2)
+            if s < last:
+                make_feature(s + 1)
             if s == PACK + 1:
                 quantise_z(0, 0, M)
                 for u in range(PIECES):

@@ -51,7 +51,6 @@ def tile_list_bearing_slot_scorer_kernel(
         wgs_sb = keep.tile([P, S], F32, name="wgs_sb")
         gain = keep.tile([P, R_PASSES, PACK], F32, name="gain")
         bias_sb = keep.tile([P, N // P], F32, name="bias_sb")
-        site_sb = [keep.tile([P, PACK, M], F32, name=f"site{b}") for b in range(R_PASSES)]
         pages = [keep.tile([P, T2], F32, name=f"page{i}") for i in range(2)]
 
         warm = keep.tile([P, 2], F32, name="warm")
@@ -101,11 +100,21 @@ def tile_list_bearing_slot_scorer_kernel(
         load_weight("w1", w1, 1, 0, 0, PASS // 2)
         load_weight("w1", w1, 1, 0, PASS // 2, PASS)
         nc.sync.dma_start(out=wgs_sb[:], in_=wgs)
-        nc.sync.dma_start(out=site_sb[0][:], in_=site[0:PASS, :].rearrange("(p t) m -> p t m", t=PACK))
-        for name, w in (("w3", w3), ("w1", w1)):
-            for a in range(K_PASSES):
-                load_weight(name, w, a, 1, 0, PASS)
-        nc.sync.dma_start(out=site_sb[1][:], in_=site[PASS : 2 * PASS, :].rearrange("(p t) m -> p t m", t=PACK))
+        site_sb = {}
+
+        def load_site(s):
+            b, t = divmod(s, PACK)
+            site_sb[s] = work.tile([P, M], F32, name=f"site{s}", tag=f"site{s}", bufs=1, align_bytes=64)
+            nc.sync.dma_start(out=site_sb[s][:], in_=site[PASS * b + t : PASS * (b + 1) : PACK, :])
+
+        load_weight("w3", w3, 0, 1, 0, PASS)
+        load_site(0)
+        load_weight("w3", w3, 1, 1, 0, PASS)
+        load_weight("w1", w1, 0, 1, 0, PASS)
+        load_site(1)
+        load_weight("w1", w1, 1, 1, 0, PASS)
+        for s in range(2, SLICES):
+            load_site(s)
         nc.sync.dma_start(
             out=w4_w[:].bitcast(I32), in_=w4_words.rearrange("b p c i -> p b (c i)").bitcast(I32)
         )
@@ -171,12 +180,14 @@ def tile_list_bearing_slot_scorer_kernel(
                     start=(a == 0), stop=(a == K_PASSES - 1),
                 )
 
-        larger, cosine, feature = {}, {}, {}
+        pair, larger, cosine, feature = {}, {}, {}, {}
 
         shared = {
             ("right", 0): "stage_a", ("larger", 0): "stage_b", ("larger", 1): "stage_c", ("feature", 0): "stage_d",
-            ("feature", PACK - 1): "stage_d",
+            ("larger", PACK - 1): "stage_d",
         }
+        for s in range(2, SLICES):
+            shared[("feature", s)] = f"site{s - 2}"
 
         def slice_tile(kind, s, bufs):
             tag, depth = (shared[(kind, s)], 1) if (kind, s) in shared else (kind, bufs)
@@ -194,15 +205,21 @@ def tile_list_bearing_slot_scorer_kernel(
             nc.scalar.activation(out=size[:], in_=phase_ps[:], func=ACT.Abs)
             cosine[s] = slice_tile("cosine", s, 3)
             nc.scalar.activation(out=cosine[s][:], in_=size[:], func=ACT.Sin, scale=-1.0, bias=math.pi / 2)
+            if s > 0:
+                nc.scalar.activation(out=cosine[s][:], in_=cosine[s][:], func=ACT.Copy, scale=gain[:, b, t : t + 1])
             left_ps = psum.tile([P, S], F32, name=f"left_ps{s}", tag="left", bufs=2)
             product(left_ps, "w1", b, t)
+            pair[s] = (left_ps, right)
+
+        def take_larger(s):
+            left_ps, right = pair[s]
             larger[s] = slice_tile("larger", s, 2)
             nc.vector.tensor_tensor(out=larger[s][:], in0=left_ps[:], in1=right[:], op=ALU.max)
 
         def make_feature(s):
             b, t = divmod(s, PACK)
             factor = slice_tile("factor", s, 1)
-            feature[s] = slice_tile("feature", s, 2)
+            feature[s] = slice_tile("feature", s, 1)
             if s == 0:
                 nc.vector.scalar_tensor_tensor(
                     out=factor[:], in0=cosine[s][:], scalar=gain[:, b, t : t + 1], in1=wgs_sb[:],
@@ -210,7 +227,6 @@ def tile_list_bearing_slot_scorer_kernel(
                 )
                 nc.vector.tensor_tensor(out=feature[s][:], in0=larger[s][:], in1=factor[:], op=ALU.mult)
             else:
-                nc.scalar.activation(out=cosine[s][:], in_=cosine[s][:], func=ACT.Copy, scale=gain[:, b, t : t + 1])
                 nc.gpsimd.tensor_tensor(out=factor[:], in0=cosine[s][:], in1=wgs_sb[:], op=ALU.mult)
                 nc.gpsimd.tensor_tensor(out=feature[s][:], in0=larger[s][:], in1=factor[:], op=ALU.mult)
 
@@ -225,7 +241,7 @@ def tile_list_bearing_slot_scorer_kernel(
                 z_f32[b] = keep.tile([P, PACK, M], F32, name=f"z_f32_{b}")
             nc.vector.tensor_tensor(
                 z_f32[b][:, t, m0:m1], pages[s % 2][:].indirect(list3[:, m0 // 16 : m1 // 16]),
-                site_sb[b][:, t, m0:m1], ALU.add,
+                site_sb[s][:, m0:m1], ALU.add,
             )
 
         z_bf16 = {}
@@ -278,17 +294,13 @@ def tile_list_bearing_slot_scorer_kernel(
             nc.sync.dma_start(out=cols.rearrange("(c p) m -> p c m", p=P), in_=score[:])
 
         readings(0)
+        take_larger(0)
         make_feature(0)
         readings(1)
+        take_larger(1)
         last = SLICES - 1
         for s in range(SLICES):
             place(s)
-            if s == 1:
-                quantise_weight("w3", 0, 1, PASS, "stage_a", 1, whole)
-                quantise_weight("w3", 1, 1, PASS, "stage_b", 1, whole)
-            if s == 2:
-                quantise_weight("w1", 0, 1, PASS, "stage_c", 1, whole)
-                quantise_weight("w1", 1, 1, PASS, "stage_d", 1, whole)
             if s < last:
                 make_feature(s + 1)
             if s == PACK + 1:
@@ -297,10 +309,18 @@ def tile_list_bearing_slot_scorer_kernel(
                     score_passes(0, u)
             if s < last:
                 fetch(s, 0, M)
-            if s + 2 < SLICES:
-                readings(s + 2)
             if s == PACK - 1:
                 round_z(0, 0, M, nc.scalar.copy)
+            if s + 2 < SLICES:
+                readings(s + 2)
+            if s == 1:
+                quantise_weight("w3", 0, 1, PASS, "stage_a", 1, whole)
+                quantise_weight("w3", 1, 1, PASS, "stage_b", 1, whole)
+                quantise_weight("w1", 0, 1, PASS, "stage_c", 1, whole)
+                quantise_weight("w1", 1, 1, PASS, "stage_d", 1, whole)
+            if s + 2 < SLICES:
+                take_larger(s + 2)
+
         def piece(u):
             return PIECE * u, PIECE * (u + 1)
 

import math
from contextlib import ExitStack

import concourse.mybir as mybir

K, T, H, S, T2, M, N = 1024, 2048, 1024, 512, 1024, 512, 512
FLOPS = 2 * (3 * K * H * S + H * N * M)

F32 = mybir.dt.float32
BF16 = mybir.dt.bfloat16
I32 = mybir.dt.int32
U32 = mybir.dt.uint32
U16 = mybir.dt.uint16
U8 = mybir.dt.uint8
FP8X4 = mybir.dt.float8_e4m3fn_x4
FP4X4 = mybir.dt.float4_e2m1fn_x4
ALU = mybir.AluOpType
ACT = mybir.ActivationFunctionType

P = 128
PACK = 4
PASS = P * PACK
K_PASSES = K // PASS
R_PASSES = H // PASS
SLICES = R_PASSES * PACK
PIECES = 4
PIECE = M // PIECES
N_TILES = N // P


def tile_list_bearing_slot_scorer_kernel(
    tc, tab_words, tab_scales, offs, offs2, offs3, w1, w2_words, w2_scales, w3, wgs, slotgain, site,
    w4_words, w4_scales, bias, out,
):
    nc = tc.nc
    with ExitStack() as ctx:
        keep = ctx.enter_context(tc.tile_pool(name="keep", bufs=1))
        work = ctx.enter_context(tc.tile_pool(name="work", bufs=1))
        psum = ctx.enter_context(tc.psum_pool(name="psum", bufs=1))

        list1 = keep.tile([P, S // 16], U16, name="list1")
        list2 = keep.tile([P, S // 16], U16, name="list2")
        list3 = keep.tile([P, M // 16], U16, name="list3")

        tab_w = [keep.tile([P, T], U32, name=f"tab_w{a}", align_bytes=64) for a in range(K_PASSES)]
        tab_s = keep.tile([P, K_PASSES, T], U8, name="tab_s", align_bytes=64)
        w2_w = [keep.tile([P, 2 * H], U8, name=f"w2_w{a}", align_bytes=64) for a in range(K_PASSES)]
        w2_s = keep.tile([P, K_PASSES, H], U8, name="w2_s", align_bytes=64)
        w4_w = keep.tile([P, R_PASSES, N], U32, name="w4_w", align_bytes=64)
        w4_s = keep.tile([P, R_PASSES, N], U8, name="w4_s", align_bytes=64)
        wgs_sb = keep.tile([P, S], F32, name="wgs_sb")
        gain = keep.tile([P, R_PASSES, PACK], F32, name="gain")
        bias_sb = keep.tile([P, N // P], F32, name="bias_sb")
        pages = [keep.tile([P, T2], F32, name=f"page{i}") for i in range(2)]

        warm = keep.tile([P, 2], F32, name="warm")
        nc.vector.memset(warm[:], 0.0)
        nc.scalar.activation(out=warm[:, 1:2], in_=warm[:, 0:1], func=ACT.Sin)
        for plane in (tab_s, w2_s, w4_s):
            nc.vector.memset(plane[:].bitcast(I32), 0)
        for page in pages:
            nc.vector.memset(page[:], 0.0)

        def load_scales(queue, plane, rows):
            for r in range(4):
                queue.dma_start(
                    out=plane[r:P:32].bitcast(I32),
                    in_=rows.bitcast(I32)[:, r:16:4, :].rearrange("a q c -> q a c"),
                )

        raw = {}

        def load_weight(name, w, a, b, c0, c1):
            tile = work.tile([P, PACK, c1 - c0], F32, name=f"raw_{name}{a}{b}{c0}", tag=f"raw{c1 - c0}", bufs=7 if c1 - c0 == PASS else 2)
            rows = w[PASS * a : PASS * (a + 1), PASS * b + c0 : PASS * b + c1]
            nc.sync.dma_start(out=tile[:], in_=rows.rearrange("(p j) c -> p j c", j=PACK))
            raw.setdefault((name, a, b), []).append((tile, c0, c1))

        def load_table(a):
            nc.sync.dma_start(
                out=tab_w[a][:].bitcast(I32), in_=tab_words[a].rearrange("p t i -> p (t i)").bitcast(I32)
            )

        def load_w2(a):
            nc.sync.dma_start(out=w2_w[a][:].bitcast(I32), in_=w2_words[a].bitcast(I32))

        nc.sync.dma_start(list1[:], offs)
        load_w2(0)
        nc.sync.dma_start(list2[:], offs2)
        nc.sync.dma_start(list3[:], offs3)
        nc.sync.dma_start(out=gain[:], in_=slotgain.rearrange("(b p t) -> p b t", b=R_PASSES, t=PACK))
        load_w2(1)
        load_table(0)
        load_table(1)
        load_scales(nc.sync, tab_s, tab_scales)
        load_weight("w3", w3, 0, 0, 0, PASS)
        load_scales(nc.sync, w2_s, w2_scales)
        load_weight("w3", w3, 1, 0, 0, PASS)
        load_weight("w1", w1, 0, 0, 0, PASS)
        load_weight("w1", w1, 1, 0, 0, PASS // 2)
        load_weight("w1", w1, 1, 0, PASS // 2, PASS)
        nc.sync.dma_start(out=wgs_sb[:], in_=wgs)
        site_sb = {}

        def load_site(s):
            b, t = divmod(s, PACK)
            site_sb[s] = work.tile([P, M], F32, name=f"site{s}", tag=f"site{s}", bufs=1, align_bytes=64)
            nc.sync.dma_start(out=site_sb[s][:], in_=site[PASS * b + t : PASS * (b + 1) : PACK, :])

        load_weight("w3", w3, 0, 1, 0, PASS)
        load_site(0)
        load_weight("w3", w3, 1, 1, 0, PASS)
        load_weight("w1", w1, 0, 1, 0, PASS)
        load_site(1)
        load_weight("w1", w1, 1, 1, 0, PASS)
        for s in range(2, SLICES):
            load_site(s)
        nc.sync.dma_start(
            out=w4_w[:].bitcast(I32), in_=w4_words.rearrange("b p c i -> p b (c i)").bitcast(I32)
        )
        load_scales(nc.sync, w4_s, w4_scales)
        with nc.allow_non_contiguous_dma(reason="one small vector laid along the partitions"):
            nc.sync.dma_start(out=bias_sb[:], in_=bias.rearrange("(c p) -> p c", p=P))

        v_w = [keep.tile([P, S], U32, name=f"v_w{a}", align_bytes=64) for a in range(K_PASSES)]
        v_s = [keep.tile([P, S], U8, name=f"v_s{a}", align_bytes=64) for a in range(K_PASSES)]

        w2_wd = keep.tile([P, K_PASSES, R_PASSES, PACK, 2 * P], U8, name="w2_wd", align_bytes=64)
        w2_sd = keep.tile([P, K_PASSES, R_PASSES, PACK, P], U8, name="w2_sd", align_bytes=64)
        for a in range(K_PASSES):
            nc.vector.tensor_copy(
                out=w2_wd[:, a].bitcast(U16).rearrange("p b (u e) q -> p b u q e", e=2),
                in_=w2_w[a][:].bitcast(U16).rearrange("p (b q u e) -> p b u q e", b=R_PASSES, u=2, e=2),
            )
        for a in range(K_PASSES):
            nc.vector.tensor_copy(v_w[a][:], tab_w[a][:].indirect(list1[:]))
        for a in range(K_PASSES):
            nc.vector.tensor_copy(v_s[a][:], tab_s[:, a, :].indirect(list1[:]))
        nc.vector.tensor_copy(
            out=w2_sd[:].rearrange("p a b (u e) q -> p (a b) u q e", e=2),
            in_=w2_s[:].rearrange("p a (b q u e) -> p (a b) u q e", b=R_PASSES, u=2, e=2),
        )

        codes = {}

        def quantise_weight(name, a, b, split, tag, bufs, cuts):
            grouped = work.tile([P, PACK, P, PACK], BF16, name=f"grp_{name}{a}{b}", tag=tag, bufs=bufs, align_bytes=64)
            for tile, c0, c1 in raw[(name, a, b)]:
                for cast, lo, hi in ((nc.scalar.copy, c0, min(c1, split)), (nc.vector.tensor_copy, max(c0, split), c1)):
                    if lo < hi:
                        cast(
                            out=grouped[:, :, lo // PACK : hi // PACK, :].rearrange("p (u e) q j -> p u q j e", e=2),
                            in_=tile[:, :, lo - c0 : hi - c0].rearrange("p j (q u e) -> p u q j e", u=2, e=2),
                        )
            words = keep.tile([P, PASS], U32, name=f"words_{name}{a}{b}", align_bytes=64)
            scales = keep.tile([P, PASS], U8, name=f"scales_{name}{a}{b}", align_bytes=64)
            for t0, t1 in cuts:
                nc.vector.quantize_mx(
                    out=words[:, P * t0 : P * t1].bitcast(FP8X4),
                    scales=scales[:, P * t0 : P * t1],
                    in_=grouped[:, t0:t1].rearrange("p t q j -> p (t q j)"),
                )
            codes[(name, a, b)] = (words, scales)

        whole = [(0, PACK)]
        quantise_weight("w3", 0, 0, PASS, "stage_c", 1, whole)
        quantise_weight("w3", 1, 0, 192, "stage_b", 1, whole)
        quantise_weight("w1", 0, 0, PASS // 2, "stage_a", 1, whole)
        quantise_weight("w1", 1, 0, 0, "stage_d", 1, [(0, 1), (1, PACK)])

        def product(acc, name, b, t):
            for a in range(K_PASSES):
                if name == "w2":
                    lhs, lhs_scale = w2_wd[:, a, b, t, :].bitcast(FP4X4), w2_sd[:, a, b, t, :]
                else:
                    words, scales = codes[(name, a, b)]
                    lhs, lhs_scale = words[:, P * t : P * (t + 1)].bitcast(FP8X4), scales[:, P * t : P * (t + 1)]
                nc.tensor.matmul_mx(
                    out=acc[:], lhsT=lhs, lhsT_scale=lhs_scale, rhs=v_w[a][:].bitcast(FP8X4), rhs_scale=v_s[a][:],
                    start=(a == 0), stop=(a == K_PASSES - 1),
                )

        pair, larger, cosine, feature = {}, {}, {}, {}

        shared = {
            ("right", 0): "stage_a", ("larger", 0): "stage_b", ("larger", 1): "stage_c", ("feature", 0): "stage_d",
            ("larger", PACK - 1): "stage_d",
        }
        for s in range(2, SLICES):
            shared[("feature", s)] = f"site{s - 2}"

        def slice_tile(kind, s, bufs):
            tag, depth = (shared[(kind, s)], 1) if (kind, s) in shared else (kind, bufs)
            return work.tile([P, S], F32, name=f"{kind}{s}", tag=tag, bufs=depth, align_bytes=64)

        def readings(s):
            b, t = divmod(s, PACK)
            right_ps = psum.tile([P, S], F32, name=f"right_ps{s}", tag="right")
            product(right_ps, "w2", b, t)
            right = slice_tile("right", s, 3)
            nc.scalar.copy(out=right[:], in_=right_ps[:])
            phase_ps = psum.tile([P, S], F32, name=f"phase_ps{s}", tag="phase")
            product(phase_ps, "w3", b, t)
            size = work.tile([P, S], F32, name=f"size{s}", tag="size", bufs=2)
            nc.scalar.activation(out=size[:], in_=phase_ps[:], func=ACT.Abs)
            cosine[s] = slice_tile("cosine", s, 3)
            nc.scalar.activation(out=cosine[s][:], in_=size[:], func=ACT.Sin, scale=-1.0, bias=math.pi / 2)
            if s > 0:
                nc.scalar.activation(out=cosine[s][:], in_=cosine[s][:], func=ACT.Copy, scale=gain[:, b, t : t + 1])
            left_ps = psum.tile([P, S], F32, name=f"left_ps{s}", tag="left", bufs=2)
            product(left_ps, "w1", b, t)
            pair[s] = (left_ps, right)

        def take_larger(s):
            left_ps, right = pair[s]
            larger[s] = slice_tile("larger", s, 2)
            nc.vector.tensor_tensor(out=larger[s][:], in0=left_ps[:], in1=right[:], op=ALU.max)

        def make_feature(s):
            b, t = divmod(s, PACK)
            factor = slice_tile("factor", s, 1)
            feature[s] = slice_tile("feature", s, 1)
            if s == 0:
                nc.vector.scalar_tensor_tensor(
                    out=factor[:], in0=cosine[s][:], scalar=gain[:, b, t : t + 1], in1=wgs_sb[:],
                    op0=ALU.mult, op1=ALU.mult,
                )
                nc.vector.tensor_tensor(out=feature[s][:], in0=larger[s][:], in1=factor[:], op=ALU.mult)
            else:
                nc.gpsimd.tensor_tensor(out=factor[:], in0=cosine[s][:], in1=wgs_sb[:], op=ALU.mult)
                nc.gpsimd.tensor_tensor(out=feature[s][:], in0=larger[s][:], in1=factor[:], op=ALU.mult)

        def place(s):
            nc.vector.tensor_copy(pages[s % 2][:].indirect(list2[:]), feature[s][:])

        z_f32 = {}

        def fetch(s, m0, m1):
            b, t = divmod(s, PACK)
            if b not in z_f32:
                z_f32[b] = keep.tile([P, PACK, M], F32, name=f"z_f32_{b}")
            nc.vector.tensor_tensor(
                z_f32[b][:, t, m0:m1], pages[s % 2][:].indirect(list3[:, m0 // 16 : m1 // 16]),
                site_sb[s][:, m0:m1], ALU.add,
            )

        z_bf16 = {}
        z_w = [keep.tile([P, M], U32, name=f"z_w{b}", align_bytes=64) for b in range(R_PASSES)]
        z_s = [keep.tile([P, M], U8, name=f"z_s{b}", align_bytes=64) for b in range(R_PASSES)]

        def round_z(b, m0, m1, cast):
            z_bf16[(b, m0)] = keep.tile([P, m1 - m0, PACK], BF16, name=f"z_bf16_{b}_{m0}", align_bytes=64)
            cast(
                out=z_bf16[(b, m0)][:].rearrange("p (c i) t -> p c t i", i=4),
                in_=z_f32[b][:, :, m0:m1].rearrange("p t (c i) -> p c t i", i=4),
            )

        def quantise_z(b, m0, m1):
            nc.vector.quantize_mx(
                out=z_w[b][:, m0:m1].bitcast(FP8X4), scales=z_s[b][:, m0:m1],
                in_=z_bf16[(b, m0)][:].rearrange("p m t -> p (m t)"),
            )

        score_ps = [psum.tile([P, N_TILES, PIECE], F32, name=f"score_ps{u}") for u in range(PIECES)]

        def score_passes(b, u):
            cols = slice(PIECE * u, PIECE * (u + 1))
            for c in range(N_TILES):
                rows = slice(P * c, P * (c + 1))
                nc.tensor.matmul_mx(
                    out=score_ps[u][:, c, :],
                    lhsT=w4_w[:, b, rows].bitcast(FP8X4), lhsT_scale=w4_s[:, b, rows],
                    rhs=z_w[b][:, cols].bitcast(FP8X4), rhs_scale=z_s[b][:, cols],
                    start=(b == 0 and c == 0), stop=(b == R_PASSES - 1 and c == N_TILES - 1),
                )

        def store_scores(u):
            score = work.tile([P, N_TILES, PIECE], F32, name=f"score{u}", tag="score", bufs=PIECES)
            if u == PIECES - 2:
                signed = work.tile([P, N_TILES, PIECE], F32, name="signed", tag="larger", bufs=2, align_bytes=64)
                nc.vector.tensor_tensor(
                    out=signed[:], in0=score_ps[u][:], in1=bias_sb[:].unsqueeze(2).to_broadcast([P, N_TILES, PIECE]),
                    op=ALU.add,
                )
                nc.vector.scalar_tensor_tensor(
                    out=score[:], in0=signed[:], scalar=-1.0, in1=signed[:], op0=ALU.mult, op1=ALU.max
                )
            else:
                for c in range(N_TILES):
                    nc.scalar.activation(
                        out=score[:, c, :], in_=score_ps[u][:, c, :], func=ACT.Abs, bias=bias_sb[:, c : c + 1]
                    )
            cols = out[:, PIECE * u : PIECE * (u + 1)]
            nc.sync.dma_start(out=cols.rearrange("(c p) m -> p c m", p=P), in_=score[:])

        readings(0)
        take_larger(0)
        make_feature(0)
        readings(1)
        take_larger(1)
        last = SLICES - 1
        for s in range(SLICES):
            place(s)
            if s < last:
                make_feature(s + 1)
            if s == PACK + 1:
                quantise_z(0, 0, M)
                for u in range(PIECES):
                    score_passes(0, u)
            if s < last:
                fetch(s, 0, M)
            if s == PACK - 1:
                round_z(0, 0, M, nc.scalar.copy)
            if s + 2 < SLICES:
                readings(s + 2)
            if s == 1:
                quantise_weight("w3", 0, 1, PASS, "stage_a", 1, whole)
                quantise_weight("w3", 1, 1, PASS, "stage_b", 1, whole)
                quantise_weight("w1", 0, 1, PASS, "stage_c", 1, whole)
                quantise_weight("w1", 1, 1, PASS, "stage_d", 1, whole)
            if s + 2 < SLICES:
                take_larger(s + 2)

        def piece(u):
            return PIECE * u, PIECE * (u + 1)

        for step in range(PIECES + 2):
            if step < PIECES:
                fetch(last, *piece(step))
                if step % 2 == 1:
                    round_z(1, *piece(step), nc.scalar.copy)
            if step % 2 == 1 and step - 1 < PIECES:
                round_z(1, *piece(step - 1), nc.vector.tensor_copy)
            if step >= 2:
                quantise_z(1, *piece(step - 2))
                score_passes(1, step - 2)
        for u in range(PIECES):
            store_scores(u)
